import numpy as np
import ml_dtypes


def mxq(x, axis, fmt="e4m3"):
    dtype, down = {"e4m3": (ml_dtypes.float8_e4m3fn, 7), "e5m2": (ml_dtypes.float8_e5m2, 14)}[fmt]
    v = np.moveaxis(np.asarray(x, np.float32).astype(ml_dtypes.bfloat16).astype(np.float64), axis, -1)
    blocks = v.reshape(v.shape[:-1] + (-1, 32))
    amax = np.abs(blocks).max(-1, keepdims=True)
    byte = np.maximum(np.where(amax > 0, np.frexp(amax)[1] - 1 + 127, 0) - down, 1)
    scale = np.exp2(byte - 127.0)
    codes = (blocks / scale).astype(np.float32).astype(dtype).astype(np.float64)
    return np.moveaxis((codes * scale).reshape(v.shape), -1, axis)


WIDE = False


def mx_kscale(k):
    if not WIDE:
        return np.ones(k)
    levels = np.array([10, -10, 5, -5, 0])
    if k % 512:
        return np.exp2(np.random.permutation(np.resize(levels, k // 32))).repeat(32)
    a = np.empty((k // 512, 16))
    for p in range(k // 512):
        a[p, :8] = np.random.permutation(np.resize(levels, 8))
        for g in range(8):
            far = levels[np.abs(levels - a[p, g]) >= 10]
            a[p, g + 8] = far[np.random.randint(len(far))]
    return np.exp2(a.ravel()).repeat(32)


def f64(x):
    return np.asarray(x).astype(np.float64)


def striped(idx):
    return np.tile(np.asarray(idx).reshape(-1, 16).T, (8, 1)).astype(np.uint16)


def unstriped(offs):
    return offs[:16].T.reshape(-1).astype(np.int64)


E2M1 = np.array([0.0, 0.5, 1.0, 1.5, 2.0, 3.0, 4.0, 6.0, -0.0, -0.5, -1.0, -1.5, -2.0, -3.0, -4.0, -6.0])


def pack_weight(w, fmt):
    k, n = w.shape
    w = f64(np.asarray(w, np.float32).astype(ml_dtypes.bfloat16)).reshape(k // 32, 32, n)
    amax = np.abs(w).max(1)
    if fmt == "e4m3":
        byte = np.frexp(amax)[1] - 1 + 127 - 7
    else:
        mant, ex = np.frexp(amax / 6.0)
        byte = np.where(mant > 0.5, ex, ex - 1) + 127
    byte = np.clip(np.where(amax > 0, byte, 1), 1, 254)
    scaled = (w * np.exp2(127.0 - byte)[:, None, :]).reshape(k, n).astype(np.float32)
    by_word = np.ascontiguousarray(scaled.reshape(k // 512, 128, 4, n).transpose(0, 1, 3, 2))
    if fmt == "e4m3":
        words = by_word.astype(ml_dtypes.float8_e4m3fn).view(np.uint8)
    else:
        c = by_word.astype(ml_dtypes.float4_e2m1fn).view(np.uint8) & 0xF
        words = (c[..., 0::2] | (c[..., 1::2] << 4)).reshape(k // 512, 128, 2 * n)
    return np.ascontiguousarray(words), np.ascontiguousarray(byte.astype(np.uint8).reshape(k // 512, 16, n))


def unpack_weight(words, scales, fmt):
    g, _, n = scales.shape
    words = np.ascontiguousarray(words).reshape(g, 128, n, -1)
    if fmt == "e4m3":
        vals = words.view(ml_dtypes.float8_e4m3fn).astype(np.float64)
    else:
        nib = np.empty((g, 128, n, 4), np.uint8)
        nib[..., 0::2] = words & 0xF
        nib[..., 1::2] = words >> 4
        vals = E2M1[nib]
    vals = vals * np.repeat(np.exp2(scales.astype(np.float64) - 127.0), 8, axis=1)[..., None]
    return vals.transpose(0, 1, 3, 2).reshape(g * 512, n)


def sigmoid(v):
    return 1.0 / (1.0 + np.exp(-v))


K, R, F, T, J, U = 512, 256, 512, 2048, 512, 1024


def setup_inputs():
    n = np.random.standard_normal
    idx = np.random.permutation(T)[:J]
    idx2 = np.random.permutation(U)[:J]
    fk = mx_kscale(K)
    ff = mx_kscale(F)
    tabp = pack_weight(n((K, T)) / fk[:, None], "e2m1")
    return {
        "tab_words": tabp[0],
        "tab_scales": tabp[1],
        "w1": (n((K, R)) * 1 / np.sqrt(K) * fk[:, None]).astype(np.float32),
        "w2": (n((K, R)) * 1 / np.sqrt(K) * fk[:, None]).astype(np.float32),
        "bias": (np.random.uniform(-0.5, 0.5, (R, 1))).astype(np.float32),
        "carry": (n((R, U)) * 0.7).astype(np.float32),
        "wo": (n((F, R)) * 1 / np.sqrt(F) * ff[:, None]).astype(np.float32),
        "dy": (n((F, J)) / ff[:, None]).astype(np.float32),
        "old": (0.5 * n((R, J))).astype(np.float32),
        "offs": striped(idx),
        "offs2": striped(idx2),
    }


def reference(tab_words, tab_scales, w1, w2, bias, carry, wo, dy, old, offs, offs2):
    idx = unstriped(offs)
    idx2 = unstriped(offs2)
    tabu = unpack_weight(tab_words, tab_scales, "e2m1")
    w1q = mxq(f64(w1), 0, "e4m3")
    tabidxg = tabu[:, idx]
    a = w1q.T @ tabidxg
    w2q = mxq(f64(w2), 0, "e4m3")
    b = w2q.T @ tabidxg
    h1 = np.tanh(a)
    gt = sigmoid(b + f64(bias))
    woq = mxq(f64(wo), 0, "e4m3")
    dyq = mxq(f64(dy), 0, "e4m3")
    c0 = woq.T @ dyq
    dgt = c0 * (h1 - f64(carry)[:, idx2])
    db = dgt * gt * (1.0 - gt)
    y = db * 4.0 + f64(old)
    return y

@@ -1,0 +1,147 @@
+from contextlib import ExitStack
+
+import concourse.mybir as mybir
+
+K, R, F, T, J, U = 512, 256, 512, 2048, 512, 1024
+FLOPS = 2 * K * R * J * 2 + 2 * F * R * J
+
+F32 = mybir.dt.float32
+BF16 = mybir.dt.bfloat16
+I32 = mybir.dt.int32
+U32 = mybir.dt.uint32
+U16 = mybir.dt.uint16
+U8 = mybir.dt.uint8
+FP8X4 = mybir.dt.float8_e4m3fn_x4
+FP4X4 = mybir.dt.float4_e2m1fn_x4
+ALU = mybir.AluOpType
+ACT = mybir.ActivationFunctionType
+
+P = 128
+PACK = 4
+HALVES = R // P
+DY_VECTOR_COLS = 320
+
+
+def weave_views(woven, raw, c0, c1):
+    dst = woven[:, c0:c1, :].rearrange("p (c i) t -> p c t i", i=4)
+    src = raw[:, :, c0:c1].rearrange("p t (c i) -> p c t i", i=4)
+    return dst, src
+
+
+def weave_scalar(nc, woven, raw, c0, c1):
+    dst, src = weave_views(woven, raw, c0, c1)
+    nc.scalar.activation(out=dst, in_=src, func=ACT.Copy)
+
+
+def weave_vector(nc, woven, raw, c0, c1):
+    dst, src = weave_views(woven, raw, c0, c1)
+    nc.vector.tensor_copy(out=dst, in_=src)
+
+
+def quantise(nc, codes, scales, woven, c0, c1):
+    nc.vector.quantize_mx(
+        out=codes[:, c0:c1].bitcast(FP8X4),
+        scales=scales[:, c0:c1],
+        in_=woven[:, c0:c1, :].rearrange("p c t -> p (c t)"),
+    )
+
+
+def tile_attend_ccarrymix_b_kernel(tc, tab_words, tab_scales, w1, w2, bias, carry, wo, dy, old, offs, offs2, out):
+    nc = tc.nc
+    with ExitStack() as ctx:
+        sb = ctx.enter_context(tc.tile_pool(name="sb", bufs=1))
+        ps = ctx.enter_context(tc.psum_pool(name="ps", bufs=1))
+
+        def mx_tiles(name, width):
+            raw = sb.tile([P, PACK, width], F32, name=name + "_raw", align_bytes=64)
+            woven = sb.tile([P, width, PACK], BF16, name=name + "_woven", align_bytes=64)
+            codes = sb.tile([P, width], U32, name=name + "_codes", align_bytes=64)
+            scales = sb.tile([P, width], U8, name=name + "_scales", align_bytes=64)
+            return raw, woven, codes, scales
+
+        list1 = sb.tile([P, J // 16], U16, name="list1")
+        list2 = sb.tile([P, J // 16], U16, name="list2")
+        words = sb.tile([P, T], U16, name="words", align_bytes=64)
+        sbytes = sb.tile([P, T], U8, name="sbytes", align_bytes=64)
+        words_g = sb.tile([P, J], U16, name="words_g", align_bytes=64)
+        sbytes_g = sb.tile([P, J], U8, name="sbytes_g", align_bytes=64)
+        w1_raw, w1_woven, w1_codes, w1_scales = mx_tiles("w1", R)
+        w2_raw, w2_woven, w2_codes, w2_scales = mx_tiles("w2", R)
+        wo_raw, wo_woven, wo_codes, wo_scales = mx_tiles("wo", R)
+        dy_raw, dy_woven, dy_codes, dy_scales = mx_tiles("dy", J)
+        carry_sb = [sb.tile([P, U], F32, name="carry%d" % h, align_bytes=64) for h in range(HALVES)]
+        old_sb = sb.tile([P, HALVES, J], F32, name="old_sb", align_bytes=64)
+        bias_sb = sb.tile([P, HALVES], F32, name="bias_sb")
+        half_bias = sb.tile([P, HALVES], F32, name="half_bias")
+
+        def f32_tiles(name):
+            return [sb.tile([P, J], F32, name="%s%d" % (name, h), align_bytes=64) for h in range(HALVES)]
+
+        def banks(name):
+            return [ps.tile([P, J], F32, name="%s%d" % (name, h)) for h in range(HALVES)]
+
+        h1, tb, sq, diff, mix, prod, res = [f32_tiles(n) for n in ("h1", "tb", "sq", "diff", "mix", "prod", "res")]
+        a_ps, b_ps, c_ps = banks("a_ps"), banks("b_ps"), banks("c_ps")
+
+        def rows4(x):
+            return x.rearrange("(p t) c -> p t c", t=PACK)
+
+        nc.vector.memset(sbytes[:].bitcast(I32), 0)
+        nc.sync.dma_start(out=list1[:], in_=offs)
+        nc.sync.dma_start(out=words[:].bitcast(I32), in_=tab_words[0].bitcast(I32))
+        for q in range(4):
+            nc.sync.dma_start(out=sbytes[q:P:32, :].bitcast(I32), in_=tab_scales[0][q:16:4, :].bitcast(I32))
+        nc.sync.dma_start(out=w1_raw[:], in_=rows4(w1))
+        nc.sync.dma_start(out=w2_raw[:], in_=rows4(w2))
+        nc.sync.dma_start(out=wo_raw[:], in_=rows4(wo))
+        nc.sync.dma_start(out=list2[:], in_=offs2)
+        nc.sync.dma_start(out=carry_sb[0][:], in_=carry[0:P, :])
+        nc.sync.dma_start(out=dy_raw[:], in_=rows4(dy))
+        nc.sync.dma_start(out=carry_sb[1][:], in_=carry[P:2 * P, :])
+        nc.sync.dma_start(out=old_sb[:], in_=old.rearrange("(h p) j -> p h j", p=P))
+        with nc.allow_non_contiguous_dma(reason="one bias value a partition and half"):
+            nc.gpsimd.dma_start(out=bias_sb[:], in_=bias.rearrange("(h p) o -> p (h o)", p=P))
+        nc.gpsimd.tensor_scalar(out=half_bias[:], in0=bias_sb[:], scalar1=0.5, scalar2=0.0, op0=ALU.mult, op1=ALU.add)
+
+        nc.vector.tensor_copy(out=words_g[:], in_=words[:].indirect(list1[:]))
+        nc.vector.tensor_copy(out=sbytes_g[:], in_=sbytes[:].indirect(list1[:]))
+
+        def product(bank, codes, scales, h, rhs, rhs_scale):
+            cols = slice(h * P, (h + 1) * P)
+            nc.tensor.matmul_mx(out=bank[:], lhsT=codes[:, cols].bitcast(FP8X4), lhsT_scale=scales[:, cols],
+                                rhs=rhs, rhs_scale=rhs_scale, start=True, stop=True)
+
+        tab_rhs = words_g[:].bitcast(FP4X4)
+        for h in range(HALVES):
+            weave_scalar(nc, w1_woven, w1_raw, h * P, (h + 1) * P)
+            quantise(nc, w1_codes, w1_scales, w1_woven, h * P, (h + 1) * P)
+            product(a_ps[h], w1_codes, w1_scales, h, tab_rhs, sbytes_g[:])
+        weave_vector(nc, w2_woven, w2_raw, 0, P)
+        weave_scalar(nc, w2_woven, w2_raw, P, R)
+        quantise(nc, w2_codes, w2_scales, w2_woven, 0, R)
+        for h in range(HALVES):
+            product(b_ps[h], w2_codes, w2_scales, h, tab_rhs, sbytes_g[:])
+        weave_vector(nc, wo_woven, wo_raw, 0, R)
+        quantise(nc, wo_codes, wo_scales, wo_woven, 0, R)
+
+        def mixed(h):
+            nc.vector.tensor_tensor(out=diff[h][:], in0=carry_sb[h][:].indirect(list2[:]), in1=h1[h][:], op=ALU.subtract)
+            nc.vector.scalar_tensor_tensor(out=mix[h][:], in0=sq[h][:], scalar=1.0, in1=diff[h][:],
+                                           op0=ALU.subtract, op1=ALU.mult)
+
+        for h in range(HALVES):
+            nc.scalar.activation(out=h1[h][:], in_=a_ps[h][:], func=ACT.Tanh)
+        for h in range(HALVES):
+            nc.scalar.activation(out=tb[h][:], in_=b_ps[h][:], func=ACT.Tanh, bias=half_bias[:, h:h + 1], scale=0.5)
+            nc.scalar.activation(out=sq[h][:], in_=tb[h][:], func=ACT.Square)
+        mixed(0)
+        weave_vector(nc, dy_woven, dy_raw, 0, DY_VECTOR_COLS)
+        weave_scalar(nc, dy_woven, dy_raw, DY_VECTOR_COLS, J)
+        quantise(nc, dy_codes, dy_scales, dy_woven, 0, J)
+        for h in range(HALVES):
+            product(c_ps[h], wo_codes, wo_scales, h, dy_codes[:].bitcast(FP8X4), dy_scales[:])
+        mixed(1)
+        for h in range(HALVES):
+            nc.vector.tensor_tensor(out=prod[h][:], in0=c_ps[h][:], in1=mix[h][:], op=ALU.mult)
+            nc.vector.tensor_tensor(out=res[h][:], in0=prod[h][:], in1=old_sb[:, h, :], op=ALU.add)
+            nc.sync.dma_start(out=out[h * P:(h + 1) * P, :], in_=res[h][:])

@@ -19,11 +19,11 @@ ACT = mybir.ActivationFunctionType
 P = 128
 PACK = 4
 HALVES = R // P
-DY_VECTOR_COLS = 320
+DY_VECTOR_COLS = 352
 
 
 def weave_views(woven, raw, c0, c1):
-    dst = woven[:, c0:c1, :].rearrange("p (c i) t -> p c t i", i=4)
+    dst = woven[:, PACK * c0:PACK * c1].rearrange("p (c i t) -> p c t i", i=4, t=PACK)
     src = raw[:, :, c0:c1].rearrange("p t (c i) -> p c t i", i=4)
     return dst, src
 
@@ -42,7 +42,7 @@ def quantise(nc, codes, scales, woven, c0, c1):
     nc.vector.quantize_mx(
         out=codes[:, c0:c1].bitcast(FP8X4),
         scales=scales[:, c0:c1],
-        in_=woven[:, c0:c1, :].rearrange("p c t -> p (c t)"),
+        in_=woven[:, PACK * c0:PACK * c1],
     )
 
 
@@ -53,22 +53,29 @@ def tile_attend_ccarrymix_b_kernel(tc, tab_words, tab_scales, w1, w2, bias, carr
         ps = ctx.enter_context(tc.psum_pool(name="ps", bufs=1))
 
         def mx_tiles(name, width):
-            raw = sb.tile([P, PACK, width], F32, name=name + "_raw", align_bytes=64)
-            woven = sb.tile([P, width, PACK], BF16, name=name + "_woven", align_bytes=64)
-            codes = sb.tile([P, width], U32, name=name + "_codes", align_bytes=64)
-            scales = sb.tile([P, width], U8, name=name + "_scales", align_bytes=64)
-            return raw, woven, codes, scales
+            raw = sb.tile([P, PACK, width], F32, name=name + "_raw", tag=name + "_raw", align_bytes=64)
+            codes = sb.tile([P, width], U32, name=name + "_codes", tag=name + "_codes", align_bytes=64)
+            return raw, codes
+
+        def woven_tile(name, width, tag):
+            return sb.tile([P, width * PACK], BF16, name=name, tag=tag, align_bytes=64)
+
+        def scale_tile(name, width, tag):
+            return sb.tile([P, width], U8, name=name, tag=tag, align_bytes=64)
 
         list1 = sb.tile([P, J // 16], U16, name="list1")
         list2 = sb.tile([P, J // 16], U16, name="list2")
         words = sb.tile([P, T], U16, name="words", align_bytes=64)
-        sbytes = sb.tile([P, T], U8, name="sbytes", align_bytes=64)
+        sbytes = sb.tile([P, T], U8, name="sbytes", tag="sbytes", align_bytes=64)
         words_g = sb.tile([P, J], U16, name="words_g", align_bytes=64)
         sbytes_g = sb.tile([P, J], U8, name="sbytes_g", align_bytes=64)
-        w1_raw, w1_woven, w1_codes, w1_scales = mx_tiles("w1", R)
-        w2_raw, w2_woven, w2_codes, w2_scales = mx_tiles("w2", R)
-        wo_raw, wo_woven, wo_codes, wo_scales = mx_tiles("wo", R)
-        dy_raw, dy_woven, dy_codes, dy_scales = mx_tiles("dy", J)
+        w1_raw, w1_codes = mx_tiles("w1", R)
+        w2_raw, w2_codes = mx_tiles("w2", R)
+        wo_raw, wo_codes = mx_tiles("wo", R)
+        dy_raw, dy_codes = mx_tiles("dy", J)
+        w2_scales = scale_tile("w2_scales", R, "w2_scales")
+        wo_scales = scale_tile("wo_scales", R, "wo_scales")
+        dy_scales = scale_tile("dy_scales", J, "dy_scales")
         carry_sb = [sb.tile([P, U], F32, name="carry%d" % h, align_bytes=64) for h in range(HALVES)]
         old_sb = sb.tile([P, HALVES, J], F32, name="old_sb", align_bytes=64)
         bias_sb = sb.tile([P, HALVES], F32, name="bias_sb")
@@ -80,15 +87,15 @@ def tile_attend_ccarrymix_b_kernel(tc, tab_words, tab_scales, w1, w2, bias, carr
         def banks(name):
             return [ps.tile([P, J], F32, name="%s%d" % (name, h)) for h in range(HALVES)]
 
-        h1, tb, sq, diff, mix, prod, res = [f32_tiles(n) for n in ("h1", "tb", "sq", "diff", "mix", "prod", "res")]
+        h1, sq, prod, res = [f32_tiles(n) for n in ("h1", "sq", "prod", "res")]
         a_ps, b_ps, c_ps = banks("a_ps"), banks("b_ps"), banks("c_ps")
 
         def rows4(x):
             return x.rearrange("(p t) c -> p t c", t=PACK)
 
         nc.vector.memset(sbytes[:].bitcast(I32), 0)
-        nc.sync.dma_start(out=list1[:], in_=offs)
         nc.sync.dma_start(out=words[:].bitcast(I32), in_=tab_words[0].bitcast(I32))
+        nc.sync.dma_start(out=list1[:], in_=offs)
         for q in range(4):
             nc.sync.dma_start(out=sbytes[q:P:32, :].bitcast(I32), in_=tab_scales[0][q:16:4, :].bitcast(I32))
         nc.sync.dma_start(out=w1_raw[:], in_=rows4(w1))
@@ -111,37 +118,59 @@ def tile_attend_ccarrymix_b_kernel(tc, tab_words, tab_scales, w1, w2, bias, carr
             nc.tensor.matmul_mx(out=bank[:], lhsT=codes[:, cols].bitcast(FP8X4), lhsT_scale=scales[:, cols],
                                 rhs=rhs, rhs_scale=rhs_scale, start=True, stop=True)
 
+        w1_scales = scale_tile("w1_scales", R, "w1_scales")
+        w1_woven = woven_tile("w1_woven", R, "w1_woven")
+        w2_woven = woven_tile("w2_woven", R, "w2_woven")
         tab_rhs = words_g[:].bitcast(FP4X4)
-        for h in range(HALVES):
-            weave_scalar(nc, w1_woven, w1_raw, h * P, (h + 1) * P)
-            quantise(nc, w1_codes, w1_scales, w1_woven, h * P, (h + 1) * P)
-            product(a_ps[h], w1_codes, w1_scales, h, tab_rhs, sbytes_g[:])
-        weave_vector(nc, w2_woven, w2_raw, 0, P)
-        weave_scalar(nc, w2_woven, w2_raw, P, R)
-        quantise(nc, w2_codes, w2_scales, w2_woven, 0, R)
-        for h in range(HALVES):
-            product(b_ps[h], w2_codes, w2_scales, h, tab_rhs, sbytes_g[:])
+        for raw, woven, codes, scales, bank in ((w1_raw, w1_woven, w1_codes, w1_scales, a_ps),
+                                                (w2_raw, w2_woven, w2_codes, w2_scales, b_ps)):
+            for h in range(HALVES):
+                weave_scalar(nc, woven, raw, h * P, (h + 1) * P)
+                quantise(nc, codes, scales, woven, h * P, (h + 1) * P)
+                product(bank[h], codes, scales, h, tab_rhs, sbytes_g[:])
+        wo_woven = woven_tile("wo_woven", R, "w2_raw")
         weave_vector(nc, wo_woven, wo_raw, 0, R)
-        quantise(nc, wo_codes, wo_scales, wo_woven, 0, R)
 
-        def mixed(h):
-            nc.vector.tensor_tensor(out=diff[h][:], in0=carry_sb[h][:].indirect(list2[:]), in1=h1[h][:], op=ALU.subtract)
-            nc.vector.scalar_tensor_tensor(out=mix[h][:], in0=sq[h][:], scalar=1.0, in1=diff[h][:],
+        def f32_tile(name, tag):
+            return sb.tile([P, J], F32, name=name, tag=tag, align_bytes=64)
+
+        def difference(h, tag):
+            diff = f32_tile("diff%d" % h, tag)
+            nc.vector.tensor_tensor(out=diff[:], in0=carry_sb[h][:].indirect(list2[:]), in1=h1[h][:], op=ALU.subtract)
+            return diff
+
+        def mixed(h, diff, tag):
+            mix = f32_tile("mix%d" % h, tag)
+            nc.vector.scalar_tensor_tensor(out=mix[:], in0=sq[h][:], scalar=1.0, in1=diff[:],
                                            op0=ALU.subtract, op1=ALU.mult)
+            return mix
 
         for h in range(HALVES):
             nc.scalar.activation(out=h1[h][:], in_=a_ps[h][:], func=ACT.Tanh)
+        tb = [f32_tile("tb%d" % h, "tb%d" % h) for h in range(HALVES)]
         for h in range(HALVES):
             nc.scalar.activation(out=tb[h][:], in_=b_ps[h][:], func=ACT.Tanh, bias=half_bias[:, h:h + 1], scale=0.5)
+        for h in range(HALVES):
             nc.scalar.activation(out=sq[h][:], in_=tb[h][:], func=ACT.Square)
-        mixed(0)
-        weave_vector(nc, dy_woven, dy_raw, 0, DY_VECTOR_COLS)
+        diff0 = difference(0, "diff0")
+        quantise(nc, wo_codes, wo_scales, wo_woven, 0, R)
+        mix0 = mixed(0, diff0, "mix0")
+        dy_woven = woven_tile("dy_woven", J, "tb0")
+        weave_vector(nc, dy_woven, dy_raw, 0, J // 2)
+        weave_vector(nc, dy_woven, dy_raw, J // 2, DY_VECTOR_COLS)
         weave_scalar(nc, dy_woven, dy_raw, DY_VECTOR_COLS, J)
-        quantise(nc, dy_codes, dy_scales, dy_woven, 0, J)
+        quantise(nc, dy_codes, dy_scales, dy_woven, 0, J // 2)
+        quantise(nc, dy_codes, dy_scales, dy_woven, J // 2, J)
         for h in range(HALVES):
             product(c_ps[h], wo_codes, wo_scales, h, dy_codes[:].bitcast(FP8X4), dy_scales[:])
-        mixed(1)
-        for h in range(HALVES):
-            nc.vector.tensor_tensor(out=prod[h][:], in0=c_ps[h][:], in1=mix[h][:], op=ALU.mult)
-            nc.vector.tensor_tensor(out=res[h][:], in0=prod[h][:], in1=old_sb[:, h, :], op=ALU.add)
-            nc.sync.dma_start(out=out[h * P:(h + 1) * P, :], in_=res[h][:])
+        diff1 = difference(1, "dy_raw")
+        nc.vector.tensor_tensor(out=prod[0][:], in0=c_ps[0][:], in1=mix0[:], op=ALU.mult)
+        mix1 = mixed(1, diff1, "dy_codes")
+        nc.vector.tensor_tensor(out=res[0][:], in0=prod[0][:], in1=old_sb[:, 0, :], op=ALU.add)
+        nc.sync.dma_start(out=out[0:P, :], in_=res[0][:])
+        parts = [slice(0, J // 2), slice(J // 2, J)]
+        for cols in parts:
+            nc.vector.tensor_tensor(out=prod[1][:, cols], in0=c_ps[1][:, cols], in1=mix1[:, cols], op=ALU.mult)
+        for cols in parts:
+            nc.vector.tensor_tensor(out=res[1][:, cols], in0=prod[1][:, cols], in1=old_sb[:, 1, cols], op=ALU.add)
+            nc.sync.dma_start(out=out[P:2 * P, cols], in_=res[1][:, cols])

@@ -3,7 +3,7 @@ from contextlib import ExitStack
 import concourse.mybir as mybir
 
 K, R, F, T, J, U = 512, 256, 512, 2048, 512, 1024
-FLOPS = 2 * K * R * J * 2 + 2 * F * R * J
+FLOPS = 2 * (2 * K * R * J) + 2 * F * R * J
 
 F32 = mybir.dt.float32
 BF16 = mybir.dt.bfloat16
@@ -18,13 +18,18 @@ ACT = mybir.ActivationFunctionType
 
 P = 128
 PACK = 4
+QUADRANT = 32
+SCALE_ROWS = 16
+LIST_COLS = J // 16
 HALVES = R // P
-DY_VECTOR_COLS = 352
+ALIGN = 64
+RUN = 4
+DY_VECTOR_COLS = 368
 
 
 def weave_views(woven, raw, c0, c1):
-    dst = woven[:, PACK * c0:PACK * c1].rearrange("p (c i t) -> p c t i", i=4, t=PACK)
-    src = raw[:, :, c0:c1].rearrange("p t (c i) -> p c t i", i=4)
+    dst = woven[:, PACK * c0:PACK * c1].rearrange("p (c i t) -> p c t i", i=RUN, t=PACK)
+    src = raw[:, :, c0:c1].rearrange("p t (c i) -> p c t i", i=RUN)
     return dst, src
 
 
@@ -46,131 +51,130 @@ def quantise(nc, codes, scales, woven, c0, c1):
     )
 
 
+def product(nc, bank, codes, scales, h, rhs, rhs_scale):
+    cols = slice(h * P, (h + 1) * P)
+    nc.tensor.matmul_mx(out=bank[:], lhsT=codes[:, cols].bitcast(FP8X4), lhsT_scale=scales[:, cols],
+                        rhs=rhs, rhs_scale=rhs_scale, start=True, stop=True)
+
+
+def by_word_rows(x):
+    return x.rearrange("(p t) c -> p t c", t=PACK)
+
+
 def tile_attend_ccarrymix_b_kernel(tc, tab_words, tab_scales, w1, w2, bias, carry, wo, dy, old, offs, offs2, out):
     nc = tc.nc
     with ExitStack() as ctx:
         sb = ctx.enter_context(tc.tile_pool(name="sb", bufs=1))
         ps = ctx.enter_context(tc.psum_pool(name="ps", bufs=1))
 
-        def mx_tiles(name, width):
-            raw = sb.tile([P, PACK, width], F32, name=name + "_raw", tag=name + "_raw", align_bytes=64)
-            codes = sb.tile([P, width], U32, name=name + "_codes", tag=name + "_codes", align_bytes=64)
-            return raw, codes
+        def sbuf(name, shape, dtype, on=None):
+            return sb.tile(shape, dtype, name=name, tag=on or name, align_bytes=ALIGN)
 
-        def woven_tile(name, width, tag):
-            return sb.tile([P, width * PACK], BF16, name=name, tag=tag, align_bytes=64)
+        def halves(name):
+            return [sbuf("%s%d" % (name, h), [P, J], F32) for h in range(HALVES)]
 
-        def scale_tile(name, width, tag):
-            return sb.tile([P, width], U8, name=name, tag=tag, align_bytes=64)
-
-        list1 = sb.tile([P, J // 16], U16, name="list1")
-        list2 = sb.tile([P, J // 16], U16, name="list2")
-        words = sb.tile([P, T], U16, name="words", align_bytes=64)
-        sbytes = sb.tile([P, T], U8, name="sbytes", tag="sbytes", align_bytes=64)
-        words_g = sb.tile([P, J], U16, name="words_g", align_bytes=64)
-        sbytes_g = sb.tile([P, J], U8, name="sbytes_g", align_bytes=64)
-        w1_raw, w1_codes = mx_tiles("w1", R)
-        w2_raw, w2_codes = mx_tiles("w2", R)
-        wo_raw, wo_codes = mx_tiles("wo", R)
-        dy_raw, dy_codes = mx_tiles("dy", J)
-        w2_scales = scale_tile("w2_scales", R, "w2_scales")
-        wo_scales = scale_tile("wo_scales", R, "wo_scales")
-        dy_scales = scale_tile("dy_scales", J, "dy_scales")
-        carry_sb = [sb.tile([P, U], F32, name="carry%d" % h, align_bytes=64) for h in range(HALVES)]
-        old_sb = sb.tile([P, HALVES, J], F32, name="old_sb", align_bytes=64)
-        bias_sb = sb.tile([P, HALVES], F32, name="bias_sb")
-        half_bias = sb.tile([P, HALVES], F32, name="half_bias")
-
-        def f32_tiles(name):
-            return [sb.tile([P, J], F32, name="%s%d" % (name, h), align_bytes=64) for h in range(HALVES)]
-
-        def banks(name):
-            return [ps.tile([P, J], F32, name="%s%d" % (name, h)) for h in range(HALVES)]
-
-        h1, sq, prod, res = [f32_tiles(n) for n in ("h1", "sq", "prod", "res")]
-        a_ps, b_ps, c_ps = banks("a_ps"), banks("b_ps"), banks("c_ps")
-
-        def rows4(x):
-            return x.rearrange("(p t) c -> p t c", t=PACK)
+        list1 = sb.tile([P, LIST_COLS], U16, name="list1")
+        list2 = sb.tile([P, LIST_COLS], U16, name="list2")
+        words = sbuf("words", [P, T], U16)
+        sbytes = sbuf("sbytes", [P, T], U8)
+        words_g = sbuf("words_g", [P, J], U16)
+        sbytes_g = sbuf("sbytes_g", [P, J], U8)
+        w1_raw, w2_raw, wo_raw = [sbuf(n + "_raw", [P, PACK, R], F32) for n in ("w1", "w2", "wo")]
+        w1_codes, w2_codes, wo_codes = [sbuf(n + "_codes", [P, R], U32) for n in ("w1", "w2", "wo")]
+        w1_scales, w2_scales, wo_scales = [sbuf(n + "_scales", [P, R], U8) for n in ("w1", "w2", "wo")]
+        w1_woven, w2_woven = [sbuf(n + "_woven", [P, PACK * R], BF16) for n in ("w1", "w2")]
+        dy_raw = sbuf("dy_raw", [P, PACK, J], F32)
+        dy_codes = sbuf("dy_codes", [P, J], U32)
+        dy_scales = sbuf("dy_scales", [P, J], U8)
+        carry_sb = [sbuf("carry%d" % h, [P, U], F32) for h in range(HALVES)]
+        old_sb = sbuf("old_sb", [P, HALVES, J], F32)
+        bias_sb = sbuf("bias_sb", [P, HALVES], F32)
+        half_bias = sbuf("half_bias", [P, HALVES], F32)
+        h1, gate_t, prod, res = halves("h1_"), halves("gate_t"), halves("prod"), halves("res")
+        a_ps = [ps.tile([P, J], F32, name="a_ps%d" % h) for h in range(HALVES)]
+        c_ps = [ps.tile([P, J], F32, name="c_ps%d" % h) for h in range(HALVES)]
 
         nc.vector.memset(sbytes[:].bitcast(I32), 0)
         nc.sync.dma_start(out=words[:].bitcast(I32), in_=tab_words[0].bitcast(I32))
         nc.sync.dma_start(out=list1[:], in_=offs)
-        for q in range(4):
-            nc.sync.dma_start(out=sbytes[q:P:32, :].bitcast(I32), in_=tab_scales[0][q:16:4, :].bitcast(I32))
-        nc.sync.dma_start(out=w1_raw[:], in_=rows4(w1))
-        nc.sync.dma_start(out=w2_raw[:], in_=rows4(w2))
-        nc.sync.dma_start(out=wo_raw[:], in_=rows4(wo))
+        for i in range(4):
+            nc.sync.dma_start(out=sbytes[i:P:QUADRANT, :].bitcast(I32),
+                              in_=tab_scales[0][i:SCALE_ROWS:4, :].bitcast(I32))
+        nc.sync.dma_start(out=w1_raw[:], in_=by_word_rows(w1))
+        nc.sync.dma_start(out=w2_raw[:], in_=by_word_rows(w2))
+        nc.sync.dma_start(out=wo_raw[:], in_=by_word_rows(wo))
         nc.sync.dma_start(out=list2[:], in_=offs2)
         nc.sync.dma_start(out=carry_sb[0][:], in_=carry[0:P, :])
-        nc.sync.dma_start(out=dy_raw[:], in_=rows4(dy))
-        nc.sync.dma_start(out=carry_sb[1][:], in_=carry[P:2 * P, :])
+        nc.sync.dma_start(out=dy_raw[:], in_=by_word_rows(dy))
+        nc.sync.dma_start(out=carry_sb[1][:], in_=carry[P:R, :])
         nc.sync.dma_start(out=old_sb[:], in_=old.rearrange("(h p) j -> p h j", p=P))
-        with nc.allow_non_contiguous_dma(reason="one bias value a partition and half"):
+        with nc.allow_non_contiguous_dma(reason="one bias value for each partition and half"):
             nc.gpsimd.dma_start(out=bias_sb[:], in_=bias.rearrange("(h p) o -> p (h o)", p=P))
         nc.gpsimd.tensor_scalar(out=half_bias[:], in0=bias_sb[:], scalar1=0.5, scalar2=0.0, op0=ALU.mult, op1=ALU.add)
 
         nc.vector.tensor_copy(out=words_g[:], in_=words[:].indirect(list1[:]))
         nc.vector.tensor_copy(out=sbytes_g[:], in_=sbytes[:].indirect(list1[:]))
-
-        def product(bank, codes, scales, h, rhs, rhs_scale):
-            cols = slice(h * P, (h + 1) * P)
-            nc.tensor.matmul_mx(out=bank[:], lhsT=codes[:, cols].bitcast(FP8X4), lhsT_scale=scales[:, cols],
-                                rhs=rhs, rhs_scale=rhs_scale, start=True, stop=True)
-
-        w1_scales = scale_tile("w1_scales", R, "w1_scales")
-        w1_woven = woven_tile("w1_woven", R, "w1_woven")
-        w2_woven = woven_tile("w2_woven", R, "w2_woven")
         tab_rhs = words_g[:].bitcast(FP4X4)
-        for raw, woven, codes, scales, bank in ((w1_raw, w1_woven, w1_codes, w1_scales, a_ps),
-                                                (w2_raw, w2_woven, w2_codes, w2_scales, b_ps)):
-            for h in range(HALVES):
-                weave_scalar(nc, woven, raw, h * P, (h + 1) * P)
-                quantise(nc, codes, scales, woven, h * P, (h + 1) * P)
-                product(bank[h], codes, scales, h, tab_rhs, sbytes_g[:])
-        wo_woven = woven_tile("wo_woven", R, "w2_raw")
+
+        for h in range(HALVES):
+            weave_scalar(nc, w1_woven, w1_raw, h * P, (h + 1) * P)
+            quantise(nc, w1_codes, w1_scales, w1_woven, h * P, (h + 1) * P)
+            product(nc, a_ps[h], w1_codes, w1_scales, h, tab_rhs, sbytes_g[:])
+        for h in range(HALVES):
+            weave_scalar(nc, w2_woven, w2_raw, h * P, (h + 1) * P)
+            quantise(nc, w2_codes, w2_scales, w2_woven, h * P, (h + 1) * P)
+        wo_woven = sbuf("wo_woven", [P, PACK * R], BF16, on="w2_raw")
         weave_vector(nc, wo_woven, wo_raw, 0, R)
 
-        def f32_tile(name, tag):
-            return sb.tile([P, J], F32, name=name, tag=tag, align_bytes=64)
+        def gate_tanh(h):
+            b_ps = ps.tile([P, J], F32, name="b_ps%d" % h, tag="b_ps")
+            product(nc, b_ps, w2_codes, w2_scales, h, tab_rhs, sbytes_g[:])
+            nc.scalar.activation(out=gate_t[h][:], in_=b_ps[:], func=ACT.Tanh, bias=half_bias[:, h:h + 1], scale=0.5)
 
-        def difference(h, tag):
-            diff = f32_tile("diff%d" % h, tag)
+        def gate_square(h, on=None):
+            square = sbuf("square%d" % h, [P, J], F32, on)
+            nc.scalar.activation(out=square[:], in_=gate_t[h][:], func=ACT.Square)
+            return square
+
+        def carry_less_h1(h, on=None):
+            diff = sbuf("diff%d" % h, [P, J], F32, on)
             nc.vector.tensor_tensor(out=diff[:], in0=carry_sb[h][:].indirect(list2[:]), in1=h1[h][:], op=ALU.subtract)
             return diff
 
-        def mixed(h, diff, tag):
-            mix = f32_tile("mix%d" % h, tag)
-            nc.vector.scalar_tensor_tensor(out=mix[:], in0=sq[h][:], scalar=1.0, in1=diff[:],
+        def mixed(h, square, diff, on=None):
+            mix = sbuf("mix%d" % h, [P, J], F32, on)
+            nc.vector.scalar_tensor_tensor(out=mix[:], in0=square[:], scalar=1.0, in1=diff[:],
                                            op0=ALU.subtract, op1=ALU.mult)
             return mix
 
         for h in range(HALVES):
             nc.scalar.activation(out=h1[h][:], in_=a_ps[h][:], func=ACT.Tanh)
-        tb = [f32_tile("tb%d" % h, "tb%d" % h) for h in range(HALVES)]
-        for h in range(HALVES):
-            nc.scalar.activation(out=tb[h][:], in_=b_ps[h][:], func=ACT.Tanh, bias=half_bias[:, h:h + 1], scale=0.5)
-        for h in range(HALVES):
-            nc.scalar.activation(out=sq[h][:], in_=tb[h][:], func=ACT.Square)
-        diff0 = difference(0, "diff0")
+        gate_tanh(0)
+        square0 = gate_square(0)
+        diff0 = carry_less_h1(0)
         quantise(nc, wo_codes, wo_scales, wo_woven, 0, R)
-        mix0 = mixed(0, diff0, "mix0")
-        dy_woven = woven_tile("dy_woven", J, "tb0")
+        mix0 = mixed(0, square0, diff0)
+        gate_tanh(1)
+
+        dy_woven = sbuf("dy_woven", [P, PACK * J], BF16, on="gate_t0")
         weave_vector(nc, dy_woven, dy_raw, 0, J // 2)
         weave_vector(nc, dy_woven, dy_raw, J // 2, DY_VECTOR_COLS)
         weave_scalar(nc, dy_woven, dy_raw, DY_VECTOR_COLS, J)
         quantise(nc, dy_codes, dy_scales, dy_woven, 0, J // 2)
         quantise(nc, dy_codes, dy_scales, dy_woven, J // 2, J)
         for h in range(HALVES):
-            product(c_ps[h], wo_codes, wo_scales, h, dy_codes[:].bitcast(FP8X4), dy_scales[:])
-        diff1 = difference(1, "dy_raw")
+            product(nc, c_ps[h], wo_codes, wo_scales, h, dy_codes[:].bitcast(FP8X4), dy_scales[:])
+
+        diff1 = carry_less_h1(1, on="dy_raw")
+        square1 = gate_square(1, on="gate_t0")
         nc.vector.tensor_tensor(out=prod[0][:], in0=c_ps[0][:], in1=mix0[:], op=ALU.mult)
-        mix1 = mixed(1, diff1, "dy_codes")
+        mix1 = mixed(1, square1, diff1, on="dy_codes")
         nc.vector.tensor_tensor(out=res[0][:], in0=prod[0][:], in1=old_sb[:, 0, :], op=ALU.add)
         nc.sync.dma_start(out=out[0:P, :], in_=res[0][:])
+
         parts = [slice(0, J // 2), slice(J // 2, J)]
         for cols in parts:
             nc.vector.tensor_tensor(out=prod[1][:, cols], in0=c_ps[1][:, cols], in1=mix1[:, cols], op=ALU.mult)
         for cols in parts:
             nc.vector.tensor_tensor(out=res[1][:, cols], in0=prod[1][:, cols], in1=old_sb[:, 1, cols], op=ALU.add)
-            nc.sync.dma_start(out=out[P:2 * P, cols], in_=res[1][:, cols])
+            nc.sync.dma_start(out=out[P:R, cols], in_=res[1][:, cols])

@@ -1,6 +1,7 @@
 from contextlib import ExitStack
 
 import concourse.mybir as mybir
+from concourse.masks import make_identity
 
 K, R, F, T, J, U = 512, 256, 512, 2048, 512, 1024
 FLOPS = 2 * (2 * K * R * J) + 2 * F * R * J
@@ -88,10 +89,11 @@ def tile_attend_ccarrymix_b_kernel(tc, tab_words, tab_scales, w1, w2, bias, carr
         dy_scales = sbuf("dy_scales", [P, J], U8)
         carry_sb = [sbuf("carry%d" % h, [P, U], F32) for h in range(HALVES)]
         old_sb = sbuf("old_sb", [P, HALVES, J], F32)
-        bias_sb = sbuf("bias_sb", [P, HALVES], F32)
-        half_bias = sbuf("half_bias", [P, HALVES], F32)
+        bias_rows = sbuf("bias_rows", [P, P], F32)
+        identity = sbuf("identity", [P, P], F32)
         h1, gate_t, prod, res = halves("h1_"), halves("gate_t"), halves("prod"), halves("res")
         a_ps = [ps.tile([P, J], F32, name="a_ps%d" % h) for h in range(HALVES)]
+        bias_ps = ps.tile([P, P], F32, name="bias_ps")
         c_ps = [ps.tile([P, J], F32, name="c_ps%d" % h) for h in range(HALVES)]
 
         nc.vector.memset(sbytes[:].bitcast(I32), 0)
@@ -108,9 +110,11 @@ def tile_attend_ccarrymix_b_kernel(tc, tab_words, tab_scales, w1, w2, bias, carr
         nc.sync.dma_start(out=dy_raw[:], in_=by_word_rows(dy))
         nc.sync.dma_start(out=carry_sb[1][:], in_=carry[P:R, :])
         nc.sync.dma_start(out=old_sb[:], in_=old.rearrange("(h p) j -> p h j", p=P))
-        with nc.allow_non_contiguous_dma(reason="one bias value for each partition and half"):
-            nc.gpsimd.dma_start(out=bias_sb[:], in_=bias.rearrange("(h p) o -> p (h o)", p=P))
-        nc.gpsimd.tensor_scalar(out=half_bias[:], in0=bias_sb[:], scalar1=0.5, scalar2=0.0, op0=ALU.mult, op1=ALU.add)
+
+        nc.gpsimd.memset(bias_rows[:], 0.0)
+        nc.gpsimd.dma_start(out=bias_rows[0:HALVES, :], in_=bias.rearrange("(h p) o -> h (p o)", p=P))
+        make_identity(nc, identity[:])
+        nc.tensor.transpose(bias_ps[:], bias_rows[:], identity[:])
 
         nc.vector.tensor_copy(out=words_g[:], in_=words[:].indirect(list1[:]))
         nc.vector.tensor_copy(out=sbytes_g[:], in_=sbytes[:].indirect(list1[:]))
@@ -123,6 +127,8 @@ def tile_attend_ccarrymix_b_kernel(tc, tab_words, tab_scales, w1, w2, bias, carr
         for h in range(HALVES):
             weave_scalar(nc, w2_woven, w2_raw, h * P, (h + 1) * P)
             quantise(nc, w2_codes, w2_scales, w2_woven, h * P, (h + 1) * P)
+        half_bias = sbuf("half_bias", [P, HALVES], F32, on="w1_raw")
+        nc.scalar.activation(out=half_bias[:], in_=bias_ps[:, 0:HALVES], func=ACT.Copy, scale=0.5)
         wo_woven = sbuf("wo_woven", [P, PACK * R], BF16, on="w2_raw")
         weave_vector(nc, wo_woven, wo_raw, 0, R)
 

from contextlib import ExitStack

import concourse.mybir as mybir
from concourse.masks import make_identity

K, R, F, T, J, U = 512, 256, 512, 2048, 512, 1024
FLOPS = 2 * (2 * K * R * J) + 2 * F * R * J

F32 = mybir.dt.float32
BF16 = mybir.dt.bfloat16
I32 = mybir.dt.int32
U32 = mybir.dt.uint32
U16 = mybir.dt.uint16
U8 = mybir.dt.uint8
FP8X4 = mybir.dt.float8_e4m3fn_x4
FP4X4 = mybir.dt.float4_e2m1fn_x4
ALU = mybir.AluOpType
ACT = mybir.ActivationFunctionType

P = 128
PACK = 4
QUADRANT = 32
SCALE_ROWS = 16
LIST_COLS = J // 16
HALVES = R // P
ALIGN = 64
RUN = 4
DY_VECTOR_COLS = 368


def weave_views(woven, raw, c0, c1):
    dst = woven[:, PACK * c0:PACK * c1].rearrange("p (c i t) -> p c t i", i=RUN, t=PACK)
    src = raw[:, :, c0:c1].rearrange("p t (c i) -> p c t i", i=RUN)
    return dst, src


def weave_scalar(nc, woven, raw, c0, c1):
    dst, src = weave_views(woven, raw, c0, c1)
    nc.scalar.activation(out=dst, in_=src, func=ACT.Copy)


def weave_vector(nc, woven, raw, c0, c1):
    dst, src = weave_views(woven, raw, c0, c1)
    nc.vector.tensor_copy(out=dst, in_=src)


def quantise(nc, codes, scales, woven, c0, c1):
    nc.vector.quantize_mx(
        out=codes[:, c0:c1].bitcast(FP8X4),
        scales=scales[:, c0:c1],
        in_=woven[:, PACK * c0:PACK * c1],
    )


def product(nc, bank, codes, scales, h, rhs, rhs_scale):
    cols = slice(h * P, (h + 1) * P)
    nc.tensor.matmul_mx(out=bank[:], lhsT=codes[:, cols].bitcast(FP8X4), lhsT_scale=scales[:, cols],
                        rhs=rhs, rhs_scale=rhs_scale, start=True, stop=True)


def by_word_rows(x):
    return x.rearrange("(p t) c -> p t c", t=PACK)


def tile_attend_ccarrymix_b_kernel(tc, tab_words, tab_scales, w1, w2, bias, carry, wo, dy, old, offs, offs2, out):
    nc = tc.nc
    with ExitStack() as ctx:
        sb = ctx.enter_context(tc.tile_pool(name="sb", bufs=1))
        ps = ctx.enter_context(tc.psum_pool(name="ps", bufs=1))

        def sbuf(name, shape, dtype, on=None):
            return sb.tile(shape, dtype, name=name, tag=on or name, align_bytes=ALIGN)

        def halves(name):
            return [sbuf("%s%d" % (name, h), [P, J], F32) for h in range(HALVES)]

        list1 = sb.tile([P, LIST_COLS], U16, name="list1")
        list2 = sb.tile([P, LIST_COLS], U16, name="list2")
        words = sbuf("words", [P, T], U16)
        sbytes = sbuf("sbytes", [P, T], U8)
        words_g = sbuf("words_g", [P, J], U16)
        sbytes_g = sbuf("sbytes_g", [P, J], U8)
        w1_raw, w2_raw, wo_raw = [sbuf(n + "_raw", [P, PACK, R], F32) for n in ("w1", "w2", "wo")]
        w1_codes, w2_codes, wo_codes = [sbuf(n + "_codes", [P, R], U32) for n in ("w1", "w2", "wo")]
        w1_scales, w2_scales, wo_scales = [sbuf(n + "_scales", [P, R], U8) for n in ("w1", "w2", "wo")]
        w1_woven, w2_woven = [sbuf(n + "_woven", [P, PACK * R], BF16) for n in ("w1", "w2")]
        dy_raw = sbuf("dy_raw", [P, PACK, J], F32)
        dy_codes = sbuf("dy_codes", [P, J], U32)
        dy_scales = sbuf("dy_scales", [P, J], U8)
        carry_sb = [sbuf("carry%d" % h, [P, U], F32) for h in range(HALVES)]
        old_sb = sbuf("old_sb", [P, HALVES, J], F32)
        bias_rows = sbuf("bias_rows", [P, P], F32)
        identity = sbuf("identity", [P, P], F32)
        h1, gate_t, prod, res = halves("h1_"), halves("gate_t"), halves("prod"), halves("res")
        a_ps = [ps.tile([P, J], F32, name="a_ps%d" % h) for h in range(HALVES)]
        bias_ps = ps.tile([P, P], F32, name="bias_ps")
        c_ps = [ps.tile([P, J], F32, name="c_ps%d" % h) for h in range(HALVES)]

        nc.vector.memset(sbytes[:].bitcast(I32), 0)
        nc.sync.dma_start(out=words[:].bitcast(I32), in_=tab_words[0].bitcast(I32))
        nc.sync.dma_start(out=list1[:], in_=offs)
        for i in range(4):
            nc.sync.dma_start(out=sbytes[i:P:QUADRANT, :].bitcast(I32),
                              in_=tab_scales[0][i:SCALE_ROWS:4, :].bitcast(I32))
        nc.sync.dma_start(out=w1_raw[:], in_=by_word_rows(w1))
        nc.sync.dma_start(out=w2_raw[:], in_=by_word_rows(w2))
        nc.sync.dma_start(out=wo_raw[:], in_=by_word_rows(wo))
        nc.sync.dma_start(out=list2[:], in_=offs2)
        nc.sync.dma_start(out=carry_sb[0][:], in_=carry[0:P, :])
        nc.sync.dma_start(out=dy_raw[:], in_=by_word_rows(dy))
        nc.sync.dma_start(out=carry_sb[1][:], in_=carry[P:R, :])
        nc.sync.dma_start(out=old_sb[:], in_=old.rearrange("(h p) j -> p h j", p=P))

        nc.gpsimd.memset(bias_rows[:], 0.0)
        nc.gpsimd.dma_start(out=bias_rows[0:HALVES, :], in_=bias.rearrange("(h p) o -> h (p o)", p=P))
        make_identity(nc, identity[:])
        nc.tensor.transpose(bias_ps[:], bias_rows[:], identity[:])

        nc.vector.tensor_copy(out=words_g[:], in_=words[:].indirect(list1[:]))
        nc.vector.tensor_copy(out=sbytes_g[:], in_=sbytes[:].indirect(list1[:]))
        tab_rhs = words_g[:].bitcast(FP4X4)

        for h in range(HALVES):
            weave_scalar(nc, w1_woven, w1_raw, h * P, (h + 1) * P)
            quantise(nc, w1_codes, w1_scales, w1_woven, h * P, (h + 1) * P)
            product(nc, a_ps[h], w1_codes, w1_scales, h, tab_rhs, sbytes_g[:])
        for h in range(HALVES):
            weave_scalar(nc, w2_woven, w2_raw, h * P, (h + 1) * P)
            quantise(nc, w2_codes, w2_scales, w2_woven, h * P, (h + 1) * P)
        half_bias = sbuf("half_bias", [P, HALVES], F32, on="w1_raw")
        nc.scalar.activation(out=half_bias[:], in_=bias_ps[:, 0:HALVES], func=ACT.Copy, scale=0.5)
        wo_woven = sbuf("wo_woven", [P, PACK * R], BF16, on="w2_raw")
        weave_vector(nc, wo_woven, wo_raw, 0, R)

        def gate_tanh(h):
            b_ps = ps.tile([P, J], F32, name="b_ps%d" % h, tag="b_ps")
            product(nc, b_ps, w2_codes, w2_scales, h, tab_rhs, sbytes_g[:])
            nc.scalar.activation(out=gate_t[h][:], in_=b_ps[:], func=ACT.Tanh, bias=half_bias[:, h:h + 1], scale=0.5)

        def gate_square(h, on=None):
            square = sbuf("square%d" % h, [P, J], F32, on)
            nc.scalar.activation(out=square[:], in_=gate_t[h][:], func=ACT.Square)
            return square

        def carry_less_h1(h, on=None):
            diff = sbuf("diff%d" % h, [P, J], F32, on)
            nc.vector.tensor_tensor(out=diff[:], in0=carry_sb[h][:].indirect(list2[:]), in1=h1[h][:], op=ALU.subtract)
            return diff

        def mixed(h, square, diff, on=None):
            mix = sbuf("mix%d" % h, [P, J], F32, on)
            nc.vector.scalar_tensor_tensor(out=mix[:], in0=square[:], scalar=1.0, in1=diff[:],
                                           op0=ALU.subtract, op1=ALU.mult)
            return mix

        for h in range(HALVES):
            nc.scalar.activation(out=h1[h][:], in_=a_ps[h][:], func=ACT.Tanh)
        gate_tanh(0)
        square0 = gate_square(0)
        diff0 = carry_less_h1(0)
        quantise(nc, wo_codes, wo_scales, wo_woven, 0, R)
        mix0 = mixed(0, square0, diff0)
        gate_tanh(1)

        dy_woven = sbuf("dy_woven", [P, PACK * J], BF16, on="gate_t0")
        weave_vector(nc, dy_woven, dy_raw, 0, J // 2)
        weave_vector(nc, dy_woven, dy_raw, J // 2, DY_VECTOR_COLS)
        weave_scalar(nc, dy_woven, dy_raw, DY_VECTOR_COLS, J)
        quantise(nc, dy_codes, dy_scales, dy_woven, 0, J // 2)
        quantise(nc, dy_codes, dy_scales, dy_woven, J // 2, J)
        for h in range(HALVES):
            product(nc, c_ps[h], wo_codes, wo_scales, h, dy_codes[:].bitcast(FP8X4), dy_scales[:])

        diff1 = carry_less_h1(1, on="dy_raw")
        square1 = gate_square(1, on="gate_t0")
        nc.vector.tensor_tensor(out=prod[0][:], in0=c_ps[0][:], in1=mix0[:], op=ALU.mult)
        mix1 = mixed(1, square1, diff1, on="dy_codes")
        nc.vector.tensor_tensor(out=res[0][:], in0=prod[0][:], in1=old_sb[:, 0, :], op=ALU.add)
        nc.sync.dma_start(out=out[0:P, :], in_=res[0][:])

        parts = [slice(0, J // 2), slice(J // 2, J)]
        for cols in parts:
            nc.vector.tensor_tensor(out=prod[1][:, cols], in0=c_ps[1][:, cols], in1=mix1[:, cols], op=ALU.mult)
        for cols in parts:
            nc.vector.tensor_tensor(out=res[1][:, cols], in0=prod[1][:, cols], in1=old_sb[:, 1, cols], op=ALU.add)
            nc.sync.dma_start(out=out[P:R, cols], in_=res[1][:, cols])
